import numpy as np
import ml_dtypes


def mxq(x, axis, fmt="e4m3"):
    dtype, down = {"e4m3": (ml_dtypes.float8_e4m3fn, 7), "e5m2": (ml_dtypes.float8_e5m2, 14)}[fmt]
    v = np.moveaxis(np.asarray(x, np.float32).astype(ml_dtypes.bfloat16).astype(np.float64), axis, -1)
    blocks = v.reshape(v.shape[:-1] + (-1, 32))
    amax = np.abs(blocks).max(-1, keepdims=True)
    byte = np.maximum(np.where(amax > 0, np.frexp(amax)[1] - 1 + 127, 0) - down, 1)
    scale = np.exp2(byte - 127.0)
    codes = (blocks / scale).astype(np.float32).astype(dtype).astype(np.float64)
    return np.moveaxis((codes * scale).reshape(v.shape), -1, axis)


WIDE = False


def mx_kscale(k):
    if not WIDE:
        return np.ones(k)
    levels = np.array([10, -10, 5, -5, 0])
    if k % 512:
        return np.exp2(np.random.permutation(np.resize(levels, k // 32))).repeat(32)
    a = np.empty((k // 512, 16))
    for p in range(k // 512):
        a[p, :8] = np.random.permutation(np.resize(levels, 8))
        for g in range(8):
            far = levels[np.abs(levels - a[p, g]) >= 10]
            a[p, g + 8] = far[np.random.randint(len(far))]
    return np.exp2(a.ravel()).repeat(32)


def f64(x):
    return np.asarray(x).astype(np.float64)


def striped(idx):
    return np.tile(idx.reshape(-1, 16).T, (8, 1)).astype(np.uint16)


def unstriped(offs):
    return offs[:16].T.reshape(-1).astype(np.int64)


def pack_weight(w):
    k, n = w.shape
    w = f64(np.asarray(w, np.float32).astype(ml_dtypes.bfloat16)).reshape(k // 32, 32, n)
    amax = np.abs(w).max(1)
    byte = np.clip(np.where(amax > 0, np.frexp(amax)[1] - 1 + 127 - 7, 1), 1, 254)
    scaled = (w * np.exp2(127.0 - byte)[:, None, :]).reshape(k, n).astype(np.float32)
    words = np.ascontiguousarray(scaled.reshape(k // 512, 128, 4, n).transpose(0, 1, 3, 2)).astype(ml_dtypes.float8_e4m3fn).view(np.uint8)
    return words, np.ascontiguousarray(byte.astype(np.uint8).reshape(k // 512, 16, n))


def unpack_weight(words, scales):
    g, p, n, _ = words.shape
    vals = np.ascontiguousarray(words).view(ml_dtypes.float8_e4m3fn).astype(np.float64) * np.repeat(np.exp2(scales.astype(np.float64) - 127.0), 8, axis=1)[..., None]
    return vals.transpose(0, 1, 3, 2).reshape(g * 512, n)


def relu(v):
    return np.maximum(v, 0.0)


K, T, E, C, N = 512, 2048, 8, 128, 512


def by_expert(wq, xq):
    return np.concatenate([wq[e].T @ xq[:, e * C:(e + 1) * C] for e in range(E)], axis=1)


def setup_inputs():
    n = np.random.standard_normal
    s = mx_kscale(K)[:, None]
    packed = [pack_weight(m) for m in n((E, K, N)) / np.sqrt(K) / s[None]]
    return {
        "xT": (n((K, T)) * s).astype(np.float32),
        "w_words": np.stack([m[0] for m in packed]),
        "w_scales": np.stack([m[1] for m in packed]),
        "b": (0.3 * n((N, E))).astype(np.float32),
        "gate": np.tile(np.random.uniform(0.2, 1.0, E * C), (N, 1)).astype(np.float32),
        "offs": striped(np.random.permutation(T)[:E * C]),
    }


def reference(xT, w_words, w_scales, b, gate, offs):
    idx = unstriped(offs)
    xq = mxq(f64(xT)[:, idx], 0, "e4m3")
    w = np.stack([unpack_weight(w_words[e], w_scales[e]) for e in range(E)])
    y = by_expert(w, xq)
    y = relu(y + np.repeat(f64(b), C, axis=1))
    out = np.zeros((N, T))
    out[:, idx] = f64(gate) * y
    return out

@@ -1,0 +1,197 @@
+from contextlib import ExitStack
+
+import concourse.mybir as mybir
+
+K, T, E, C, N = 512, 2048, 8, 128, 512
+FLOPS = 2 * K * N * E * C
+
+F32 = mybir.dt.float32
+BF16 = mybir.dt.bfloat16
+I32 = mybir.dt.int32
+U32 = mybir.dt.uint32
+U16 = mybir.dt.uint16
+U8 = mybir.dt.uint8
+FP8X4 = mybir.dt.float8_e4m3fn_x4
+MULT = mybir.AluOpType.mult
+RELU = mybir.ActivationFunctionType.Relu
+
+P = 128
+PACK = 4
+SLOTS = E * C
+CHUNK = 256
+CHUNKS = SLOTS // CHUNK
+EXPERTS_PER_CHUNK = CHUNK // C
+HALF = 512
+BLOCKS = N // P
+
+
+def tile_routed_moe_kernel(tc, xT, w_words, w_scales, b, gate, offs, out):
+    nc = tc.nc
+    with ExitStack() as ctx:
+        lists = ctx.enter_context(tc.tile_pool(name="lists", bufs=1))
+        keep = ctx.enter_context(tc.tile_pool(name="keep", bufs=1))
+        psum = ctx.enter_context(tc.psum_pool(name="psum", bufs=1))
+
+        offsets = lists.tile([P, SLOTS // 16], U16, name="offsets")
+        nc.sync.dma_start(offsets[:], offs)
+
+        x_rows = xT.rearrange("(p t) n -> p t n", t=PACK)
+        planes = []
+        for t in range(PACK):
+            plane = keep.tile([P, T], F32, name="plane%d" % t)
+            nc.sync.dma_start(plane[:], x_rows[:, t, :])
+            planes.append(plane)
+
+        w_planes = keep.tile([P, E, N], U8, name="w_planes", align_bytes=64)
+        nc.vector.memset(w_planes[:].rearrange("p e n -> p (e n)").bitcast(I32), 0)
+        scale_rows = w_scales[:, 0].rearrange("e (q r) n -> r q e n", r=4)
+        for r in range(4):
+            nc.sync.dma_start(w_planes[r:P:32, :, :].bitcast(I32), scale_rows[r].bitcast(I32))
+
+        bias = keep.tile([P, BLOCKS, E], F32, name="bias")
+        gate_rows = gate.rearrange("(m p) j -> p m j", p=P)
+        w_codes = []
+        gates = []
+        for c in range(CHUNKS):
+            codes = keep.tile([P, EXPERTS_PER_CHUNK, N], U32, name="w_codes%d" % c, align_bytes=64)
+            e0 = c * EXPERTS_PER_CHUNK
+            nc.sync.dma_start(
+                codes[:].bitcast(I32),
+                w_words[e0 : e0 + EXPERTS_PER_CHUNK, 0].rearrange("e p n r -> p e (n r)").bitcast(I32),
+            )
+            w_codes.append(codes)
+            if c == 0:
+                nc.sync.dma_start(bias[:], b.rearrange("(m p) e -> p m e", p=P))
+            g = keep.tile([P, BLOCKS, CHUNK], F32, name="gate%d" % c)
+            nc.sync.dma_start(g[:], gate_rows[:, :, c * CHUNK : (c + 1) * CHUNK])
+            gates.append(g)
+
+        warm = keep.tile([P, 1], F32, name="warm")
+        warmed = keep.tile([P, 1], F32, name="warmed")
+        nc.vector.memset(warm[:], 0.0)
+        nc.scalar.activation(out=warmed[:], in_=warm[:], func=RELU)
+
+        windows = []
+        for m in range(BLOCKS):
+            window = keep.tile([P, T], F32, name="window%d" % m)
+            nc.vector.memset(window[:], 0.0)
+            windows.append(window)
+
+        picked = [keep.tile([P, PACK, HALF], F32, name="picked%d" % h) for h in range(SLOTS // HALF)]
+
+        def gather(t, j0, n):
+            h, off = divmod(j0, HALF)
+            nc.vector.tensor_copy(
+                out=picked[h][:, t, off : off + n],
+                in_=planes[t][:].indirect(offsets[:, j0 // 16 : (j0 + n) // 16]),
+            )
+
+        grouped = [keep.tile([P, CHUNK, PACK], BF16, name="grouped%d" % c, align_bytes=64) for c in range(CHUNKS)]
+        x_codes = [keep.tile([P, CHUNK], U32, name="x_codes%d" % c, align_bytes=64) for c in range(CHUNKS)]
+        x_planes = [keep.tile([P, CHUNK], U8, name="x_planes%d" % c, align_bytes=64) for c in range(CHUNKS)]
+        y = [keep.tile([P, BLOCKS, CHUNK], F32, name="y%d" % c) for c in range(CHUNKS)]
+
+        def interleave(c):
+            h, off = divmod(c * CHUNK, HALF)
+            nc.scalar.copy(out=grouped[c][:], in_=picked[h][:, :, off : off + CHUNK].rearrange("p t n -> p n t"))
+
+        def quantise(c):
+            nc.vector.quantize_mx(
+                out=x_codes[c][:].bitcast(FP8X4),
+                scales=x_planes[c][:],
+                in_=grouped[c][:].rearrange("p n t -> p (n t)"),
+            )
+
+        def multiply(c):
+            for pair in range(BLOCKS // 2):
+                acc = psum.tile([P, 2, EXPERTS_PER_CHUNK, C], F32, name="acc%d_%d" % (c, pair))
+                for s in range(2):
+                    m = 2 * pair + s
+                    for i in range(EXPERTS_PER_CHUNK):
+                        e = c * EXPERTS_PER_CHUNK + i
+                        nc.tensor.matmul_mx(
+                            out=acc[:, s, i, :],
+                            lhsT=w_codes[c][:, i, m * P : (m + 1) * P].bitcast(FP8X4),
+                            lhsT_scale=w_planes[:, e, m * P : (m + 1) * P],
+                            rhs=x_codes[c][:, i * C : (i + 1) * C].bitcast(FP8X4),
+                            rhs_scale=x_planes[c][:, i * C : (i + 1) * C],
+                            start=True,
+                            stop=True,
+                        )
+                for s in range(2):
+                    m = 2 * pair + s
+                    for i in range(EXPERTS_PER_CHUNK):
+                        e = c * EXPERTS_PER_CHUNK + i
+                        nc.scalar.activation(
+                            out=y[c][:, m, i * C : (i + 1) * C],
+                            in_=acc[:, s, i, :],
+                            func=RELU,
+                            bias=bias[:, m, e : e + 1],
+                            scale=1.0,
+                        )
+
+        weighted = [keep.tile([P, BLOCKS, CHUNK], F32, name="weighted%d" % c) for c in range(CHUNKS)]
+
+        def weigh(c, pair):
+            blocks = slice(2 * pair, 2 * pair + 2)
+            nc.vector.tensor_tensor(
+                out=weighted[c][:, blocks, :], in0=y[c][:, blocks, :], in1=gates[c][:, blocks, :], op=MULT
+            )
+
+        def put_back(c, m):
+            nc.vector.tensor_copy(
+                out=windows[m][:].indirect(offsets[:, c * CHUNK // 16 : (c + 1) * CHUNK // 16]),
+                in_=weighted[c][:, m, :],
+            )
+
+        out_blocks = out.rearrange("(m p) t -> m p t", p=P)
+
+        def store(m):
+            nc.sync.dma_start(out_blocks[m], windows[m][:])
+
+        for t in range(PACK - 1):
+            for j0 in range(0, SLOTS, HALF):
+                gather(t, j0, HALF)
+
+        gather(3, 0 * CHUNK, CHUNK)
+        interleave(0)
+        gather(3, 1 * CHUNK, CHUNK)
+        interleave(1)
+        gather(3, 2 * CHUNK, CHUNK)
+        quantise(0)
+        multiply(0)
+        gather(3, 3 * CHUNK, CHUNK)
+        interleave(2)
+        quantise(1)
+        multiply(1)
+        weigh(0, 0)
+        weigh(0, 1)
+        put_back(0, 0)
+        put_back(0, 1)
+        interleave(3)
+        quantise(2)
+        multiply(2)
+        put_back(0, 2)
+        put_back(0, 3)
+        quantise(3)
+        multiply(3)
+        weigh(1, 0)
+        weigh(1, 1)
+        put_back(1, 0)
+        put_back(1, 1)
+        weigh(2, 0)
+        put_back(1, 2)
+        weigh(3, 0)
+        put_back(1, 3)
+        put_back(2, 0)
+        put_back(3, 0)
+        store(0)
+        weigh(2, 1)
+        put_back(2, 1)
+        weigh(3, 1)
+        put_back(3, 1)
+        store(1)
+        for m in (2, 3):
+            put_back(2, m)
+            put_back(3, m)
+            store(m)

@@ -130,18 +130,12 @@ def tile_routed_moe_kernel(tc, xT, w_words, w_scales, b, gate, offs, out):
                             scale=1.0,
                         )
 
-        weighted = [keep.tile([P, BLOCKS, CHUNK], F32, name="weighted%d" % c) for c in range(CHUNKS)]
-
-        def weigh(c, pair):
-            blocks = slice(2 * pair, 2 * pair + 2)
-            nc.vector.tensor_tensor(
-                out=weighted[c][:, blocks, :], in0=y[c][:, blocks, :], in1=gates[c][:, blocks, :], op=MULT
-            )
-
         def put_back(c, m):
-            nc.vector.tensor_copy(
+            nc.vector.tensor_tensor(
                 out=windows[m][:].indirect(offsets[:, c * CHUNK // 16 : (c + 1) * CHUNK // 16]),
-                in_=weighted[c][:, m, :],
+                in0=y[c][:, m, :],
+                in1=gates[c][:, m, :],
+                op=MULT,
             )
 
         out_blocks = out.rearrange("(m p) t -> m p t", p=P)
@@ -164,8 +158,6 @@ def tile_routed_moe_kernel(tc, xT, w_words, w_scales, b, gate, offs, out):
         interleave(2)
         quantise(1)
         multiply(1)
-        weigh(0, 0)
-        weigh(0, 1)
         put_back(0, 0)
         put_back(0, 1)
         interleave(3)
@@ -175,23 +167,9 @@ def tile_routed_moe_kernel(tc, xT, w_words, w_scales, b, gate, offs, out):
         put_back(0, 3)
         quantise(3)
         multiply(3)
-        weigh(1, 0)
-        weigh(1, 1)
-        put_back(1, 0)
-        put_back(1, 1)
-        weigh(2, 0)
-        put_back(1, 2)
-        weigh(3, 0)
-        put_back(1, 3)
-        put_back(2, 0)
-        put_back(3, 0)
-        store(0)
-        weigh(2, 1)
-        put_back(2, 1)
-        weigh(3, 1)
-        put_back(3, 1)
-        store(1)
-        for m in (2, 3):
+        for m in range(BLOCKS):
+            put_back(1, m)
+        for m in range(BLOCKS):
             put_back(2, m)
             put_back(3, m)
             store(m)

@@ -48,34 +48,41 @@ def tile_routed_moe_kernel(tc, xT, w_words, w_scales, b, gate, offs, out):
         for r in range(4):
             nc.sync.dma_start(w_planes[r:P:32, :, :].bitcast(I32), scale_rows[r].bitcast(I32))
 
-        bias = keep.tile([P, BLOCKS, E], F32, name="bias")
-        gate_rows = gate.rearrange("(m p) j -> p m j", p=P)
-        w_codes = []
-        gates = []
-        for c in range(CHUNKS):
-            codes = keep.tile([P, EXPERTS_PER_CHUNK, N], U32, name="w_codes%d" % c, align_bytes=64)
+        w_codes = [keep.tile([P, EXPERTS_PER_CHUNK, N], U32, name="w_codes%d" % c, align_bytes=64) for c in range(CHUNKS)]
+
+        def load_codes(c):
             e0 = c * EXPERTS_PER_CHUNK
             nc.sync.dma_start(
-                codes[:].bitcast(I32),
+                w_codes[c][:].bitcast(I32),
                 w_words[e0 : e0 + EXPERTS_PER_CHUNK, 0].rearrange("e p n r -> p e (n r)").bitcast(I32),
             )
-            w_codes.append(codes)
-            if c == 0:
-                nc.sync.dma_start(bias[:], b.rearrange("(m p) e -> p m e", p=P))
-            g = keep.tile([P, BLOCKS, CHUNK], F32, name="gate%d" % c)
-            nc.sync.dma_start(g[:], gate_rows[:, :, c * CHUNK : (c + 1) * CHUNK])
-            gates.append(g)
 
-        warm = keep.tile([P, 1], F32, name="warm")
-        warmed = keep.tile([P, 1], F32, name="warmed")
-        nc.vector.memset(warm[:], 0.0)
-        nc.scalar.activation(out=warmed[:], in_=warm[:], func=RELU)
+        groups = [(0, CHUNK), (CHUNK, CHUNK), (2 * CHUNK, 2 * CHUNK)]
+        gate_rows = gate.rearrange("(m p) j -> p m j", p=P)
+        gates = [keep.tile([P, BLOCKS, n], F32, name="gate%d" % k) for k, (j0, n) in enumerate(groups)]
+        y = [keep.tile([P, BLOCKS, n], F32, name="y%d" % k) for k, (j0, n) in enumerate(groups)]
 
-        windows = []
-        for m in range(BLOCKS):
-            window = keep.tile([P, T], F32, name="window%d" % m)
-            nc.vector.memset(window[:], 0.0)
-            windows.append(window)
+        def load_gate(k):
+            j0, n = groups[k]
+            nc.sync.dma_start(gates[k][:], gate_rows[:, :, j0 : j0 + n])
+
+        bias = keep.tile([P, BLOCKS, E], F32, name="bias")
+        load_codes(0)
+        nc.sync.dma_start(bias[:], b.rearrange("(m p) e -> p m e", p=P))
+        load_gate(0)
+        load_codes(1)
+        load_gate(1)
+        load_codes(2)
+        load_codes(3)
+        load_gate(2)
+
+        zero = keep.tile([P, 1], F32, name="zero")
+        nc.vector.memset(zero[:], 0.0)
+        windows = [keep.tile([P, T], F32, name="window%d" % m) for m in range(BLOCKS)]
+        for m in (0, 1):
+            nc.gpsimd.memset(windows[m][:], 0.0)
+        for m in (2, 3):
+            nc.scalar.copy(out=windows[m][:], in_=zero[:, 0:1].to_broadcast([P, T]))
 
         picked = [keep.tile([P, PACK, HALF], F32, name="picked%d" % h) for h in range(SLOTS // HALF)]
 
@@ -89,11 +96,13 @@ def tile_routed_moe_kernel(tc, xT, w_words, w_scales, b, gate, offs, out):
         grouped = [keep.tile([P, CHUNK, PACK], BF16, name="grouped%d" % c, align_bytes=64) for c in range(CHUNKS)]
         x_codes = [keep.tile([P, CHUNK], U32, name="x_codes%d" % c, align_bytes=64) for c in range(CHUNKS)]
         x_planes = [keep.tile([P, CHUNK], U8, name="x_planes%d" % c, align_bytes=64) for c in range(CHUNKS)]
-        y = [keep.tile([P, BLOCKS, CHUNK], F32, name="y%d" % c) for c in range(CHUNKS)]
 
-        def interleave(c):
+        def interleave(c, t0):
             h, off = divmod(c * CHUNK, HALF)
-            nc.scalar.copy(out=grouped[c][:], in_=picked[h][:, :, off : off + CHUNK].rearrange("p t n -> p n t"))
+            nc.scalar.copy(
+                out=grouped[c][:, :, t0 : t0 + 2],
+                in_=picked[h][:, t0 : t0 + 2, off : off + CHUNK].rearrange("p t n -> p n t"),
+            )
 
         def quantise(c):
             nc.vector.quantize_mx(
@@ -103,6 +112,8 @@ def tile_routed_moe_kernel(tc, xT, w_words, w_scales, b, gate, offs, out):
             )
 
         def multiply(c):
+            k = min(c, 2)
+            col0 = c * CHUNK - groups[k][0]
             for pair in range(BLOCKS // 2):
                 acc = psum.tile([P, 2, EXPERTS_PER_CHUNK, C], F32, name="acc%d_%d" % (c, pair))
                 for s in range(2):
@@ -123,53 +134,54 @@ def tile_routed_moe_kernel(tc, xT, w_words, w_scales, b, gate, offs, out):
                     for i in range(EXPERTS_PER_CHUNK):
                         e = c * EXPERTS_PER_CHUNK + i
                         nc.scalar.activation(
-                            out=y[c][:, m, i * C : (i + 1) * C],
+                            out=y[k][:, m, col0 + i * C : col0 + (i + 1) * C],
                             in_=acc[:, s, i, :],
                             func=RELU,
                             bias=bias[:, m, e : e + 1],
                             scale=1.0,
                         )
 
-        def put_back(c, m):
+        def put_back(k, m):
+            j0, n = groups[k]
             nc.vector.tensor_tensor(
-                out=windows[m][:].indirect(offsets[:, c * CHUNK // 16 : (c + 1) * CHUNK // 16]),
-                in0=y[c][:, m, :],
-                in1=gates[c][:, m, :],
+                out=windows[m][:].indirect(offsets[:, j0 // 16 : (j0 + n) // 16]),
+                in0=y[k][:, m, :],
+                in1=gates[k][:, m, :],
                 op=MULT,
             )
 
         out_blocks = out.rearrange("(m p) t -> m p t", p=P)
 
-        def store(m):
-            nc.sync.dma_start(out_blocks[m], windows[m][:])
-
-        for t in range(PACK - 1):
+        for t in (0, 1):
             for j0 in range(0, SLOTS, HALF):
                 gather(t, j0, HALF)
+        for c in range(CHUNKS):
+            interleave(c, 0)
+        for j0 in range(0, SLOTS, HALF):
+            gather(2, j0, HALF)
 
         gather(3, 0 * CHUNK, CHUNK)
-        interleave(0)
+        interleave(0, 2)
         gather(3, 1 * CHUNK, CHUNK)
-        interleave(1)
+        interleave(1, 2)
         gather(3, 2 * CHUNK, CHUNK)
         quantise(0)
         multiply(0)
         gather(3, 3 * CHUNK, CHUNK)
-        interleave(2)
         quantise(1)
         multiply(1)
+        interleave(2, 2)
         put_back(0, 0)
         put_back(0, 1)
-        interleave(3)
         quantise(2)
         multiply(2)
+        interleave(3, 2)
         put_back(0, 2)
-        put_back(0, 3)
         quantise(3)
         multiply(3)
+        put_back(0, 3)
         for m in range(BLOCKS):
             put_back(1, m)
         for m in range(BLOCKS):
             put_back(2, m)
-            put_back(3, m)
-            store(m)
+            nc.sync.dma_start(out_blocks[m], windows[m][:])

@@ -14,6 +14,7 @@ U8 = mybir.dt.uint8
 FP8X4 = mybir.dt.float8_e4m3fn_x4
 MULT = mybir.AluOpType.mult
 RELU = mybir.ActivationFunctionType.Relu
+COPY = mybir.ActivationFunctionType.Copy
 
 P = 128
 PACK = 4
@@ -79,109 +80,112 @@ def tile_routed_moe_kernel(tc, xT, w_words, w_scales, b, gate, offs, out):
         zero = keep.tile([P, 1], F32, name="zero")
         nc.vector.memset(zero[:], 0.0)
         windows = [keep.tile([P, T], F32, name="window%d" % m) for m in range(BLOCKS)]
-        for m in (0, 1):
+        nc.vector.memset(windows[0][:], 0.0)
+        for m in (1, 2):
             nc.gpsimd.memset(windows[m][:], 0.0)
-        for m in (2, 3):
-            nc.scalar.copy(out=windows[m][:], in_=zero[:, 0:1].to_broadcast([P, T]))
+        nc.scalar.copy(out=windows[3][:], in_=zero[:, 0:1].to_broadcast([P, T]))
 
-        picked = [keep.tile([P, PACK, HALF], F32, name="picked%d" % h) for h in range(SLOTS // HALF)]
+        grouped01 = keep.tile([P, HALF, PACK], BF16, name="grouped01", align_bytes=64)
+        x_codes = [
+            keep.tile([P, CHUNK], U32, name="x_codes%d" % c, tag=("turn%d" % c if c < 2 else "x_codes%d" % c), align_bytes=64)
+            for c in range(CHUNKS)
+        ]
+        late = {}
+        x_planes = [keep.tile([P, CHUNK], U8, name="x_planes%d" % c, align_bytes=64) for c in range(CHUNKS)]
+        rounded = [keep.tile([P, T], BF16, name="rounded%d" % t) for t in range(PACK)]
 
-        def gather(t, j0, n):
-            h, off = divmod(j0, HALF)
+        def vector_gather(t, j0, n):
             nc.vector.tensor_copy(
-                out=picked[h][:, t, off : off + n],
+                out=grouped01[:, j0 : j0 + n, t],
                 in_=planes[t][:].indirect(offsets[:, j0 // 16 : (j0 + n) // 16]),
             )
 
-        grouped = [keep.tile([P, CHUNK, PACK], BF16, name="grouped%d" % c, align_bytes=64) for c in range(CHUNKS)]
-        x_codes = [keep.tile([P, CHUNK], U32, name="x_codes%d" % c, align_bytes=64) for c in range(CHUNKS)]
-        x_planes = [keep.tile([P, CHUNK], U8, name="x_planes%d" % c, align_bytes=64) for c in range(CHUNKS)]
+        def cast(t):
+            nc.scalar.copy(out=rounded[t][:], in_=planes[t][:])
 
-        def interleave(c, t0):
-            h, off = divmod(c * CHUNK, HALF)
-            nc.scalar.copy(
-                out=grouped[c][:, :, t0 : t0 + 2],
-                in_=picked[h][:, t0 : t0 + 2, off : off + CHUNK].rearrange("p t n -> p n t"),
-            )
+        def scalar_gathers(c):
+            late[c] = keep.tile([P, CHUNK, PACK], BF16, name="late%d" % c, tag="turn%d" % (c - 2), align_bytes=64)
+            for t in range(PACK):
+                nc.scalar.activation(
+                    out=late[c][:, :, t],
+                    in_=rounded[t][:].indirect(offsets[:, c * CHUNK // 16 : (c + 1) * CHUNK // 16]),
+                    func=COPY,
+                )
 
         def quantise(c):
+            values = grouped01[:, c * CHUNK : (c + 1) * CHUNK, :] if c < 2 else late[c][:]
             nc.vector.quantize_mx(
                 out=x_codes[c][:].bitcast(FP8X4),
                 scales=x_planes[c][:],
-                in_=grouped[c][:].rearrange("p n t -> p (n t)"),
+                in_=values.rearrange("p n t -> p (n t)"),
             )
 
+        sums = {}
+
         def multiply(c):
+            for m in range(BLOCKS):
+                acc = psum.tile([P, EXPERTS_PER_CHUNK, C], F32, name="acc%d_%d" % (c % 2, m))
+                sums[(c, m)] = acc
+                for i in range(EXPERTS_PER_CHUNK):
+                    e = c * EXPERTS_PER_CHUNK + i
+                    nc.tensor.matmul_mx(
+                        out=acc[:, i, :],
+                        lhsT=w_codes[c][:, i, m * P : (m + 1) * P].bitcast(FP8X4),
+                        lhsT_scale=w_planes[:, e, m * P : (m + 1) * P],
+                        rhs=x_codes[c][:, i * C : (i + 1) * C].bitcast(FP8X4),
+                        rhs_scale=x_planes[c][:, i * C : (i + 1) * C],
+                        start=True,
+                        stop=True,
+                    )
+
+        def bias_relu(c):
             k = min(c, 2)
             col0 = c * CHUNK - groups[k][0]
-            for pair in range(BLOCKS // 2):
-                acc = psum.tile([P, 2, EXPERTS_PER_CHUNK, C], F32, name="acc%d_%d" % (c, pair))
-                for s in range(2):
-                    m = 2 * pair + s
-                    for i in range(EXPERTS_PER_CHUNK):
-                        e = c * EXPERTS_PER_CHUNK + i
-                        nc.tensor.matmul_mx(
-                            out=acc[:, s, i, :],
-                            lhsT=w_codes[c][:, i, m * P : (m + 1) * P].bitcast(FP8X4),
-                            lhsT_scale=w_planes[:, e, m * P : (m + 1) * P],
-                            rhs=x_codes[c][:, i * C : (i + 1) * C].bitcast(FP8X4),
-                            rhs_scale=x_planes[c][:, i * C : (i + 1) * C],
-                            start=True,
-                            stop=True,
-                        )
-                for s in range(2):
-                    m = 2 * pair + s
-                    for i in range(EXPERTS_PER_CHUNK):
-                        e = c * EXPERTS_PER_CHUNK + i
-                        nc.scalar.activation(
-                            out=y[k][:, m, col0 + i * C : col0 + (i + 1) * C],
-                            in_=acc[:, s, i, :],
-                            func=RELU,
-                            bias=bias[:, m, e : e + 1],
-                            scale=1.0,
-                        )
+            for m in range(BLOCKS):
+                acc = sums[(c, m)]
+                for i in range(EXPERTS_PER_CHUNK):
+                    e = c * EXPERTS_PER_CHUNK + i
+                    nc.scalar.activation(
+                        out=y[k][:, m, col0 + i * C : col0 + (i + 1) * C],
+                        in_=acc[:, i, :],
+                        func=RELU,
+                        bias=bias[:, m, e : e + 1],
+                        scale=1.0,
+                    )
 
-        def put_back(k, m):
-            j0, n = groups[k]
+        def put_back(k, m, first=0, n=None):
+            n = groups[k][1] if n is None else n
+            j0 = groups[k][0] + first
             nc.vector.tensor_tensor(
                 out=windows[m][:].indirect(offsets[:, j0 // 16 : (j0 + n) // 16]),
-                in0=y[k][:, m, :],
-                in1=gates[k][:, m, :],
+                in0=y[k][:, m, first : first + n],
+                in1=gates[k][:, m, first : first + n],
                 op=MULT,
             )
 
         out_blocks = out.rearrange("(m p) t -> m p t", p=P)
 
-        for t in (0, 1):
-            for j0 in range(0, SLOTS, HALF):
-                gather(t, j0, HALF)
-        for c in range(CHUNKS):
-            interleave(c, 0)
-        for j0 in range(0, SLOTS, HALF):
-            gather(2, j0, HALF)
-
-        gather(3, 0 * CHUNK, CHUNK)
-        interleave(0, 2)
-        gather(3, 1 * CHUNK, CHUNK)
-        interleave(1, 2)
-        gather(3, 2 * CHUNK, CHUNK)
-        quantise(0)
-        multiply(0)
-        gather(3, 3 * CHUNK, CHUNK)
-        quantise(1)
-        multiply(1)
-        interleave(2, 2)
-        put_back(0, 0)
-        put_back(0, 1)
-        quantise(2)
-        multiply(2)
-        interleave(3, 2)
-        put_back(0, 2)
-        quantise(3)
-        multiply(3)
-        put_back(0, 3)
+        for t in (0, 1, 2):
+            vector_gather(t, 0, HALF)
+            cast(t)
+        cast(3)
+        vector_gather(3, 0, HALF)
+        for c in (0, 1):
+            quantise(c)
+            multiply(c)
+            bias_relu(c)
+        for c in (2, 3):
+            scalar_gathers(c)
+            quantise(c)
+            multiply(c)
+            bias_relu(c)
+        for k in (0, 1):
+            for m in range(BLOCKS):
+                put_back(k, m)
         for m in range(BLOCKS):
-            put_back(1, m)
-        for m in range(BLOCKS):
-            put_back(2, m)
+            if m == 0:
+                put_back(2, m, 0, CHUNK)
+                put_back(2, m, CHUNK, CHUNK)
+            else:
+                put_back(2, m)
             nc.sync.dma_start(out_blocks[m], windows[m][:])

@@ -78,10 +78,9 @@ def tile_routed_moe_kernel(tc, xT, w_words, w_scales, b, gate, offs, out):
         load_gate(2)
 
         zero = keep.tile([P, 1], F32, name="zero")
-        nc.vector.memset(zero[:], 0.0)
+        nc.gpsimd.memset(zero[:], 0.0)
         windows = [keep.tile([P, T], F32, name="window%d" % m) for m in range(BLOCKS)]
-        nc.vector.memset(windows[0][:], 0.0)
-        for m in (1, 2):
+        for m in (0, 1, 2):
             nc.gpsimd.memset(windows[m][:], 0.0)
         nc.scalar.copy(out=windows[3][:], in_=zero[:, 0:1].to_broadcast([P, T]))
 

@@ -46,8 +46,10 @@ def tile_routed_moe_kernel(tc, xT, w_words, w_scales, b, gate, offs, out):
         w_planes = keep.tile([P, E, N], U8, name="w_planes", align_bytes=64)
         nc.vector.memset(w_planes[:].rearrange("p e n -> p (e n)").bitcast(I32), 0)
         scale_rows = w_scales[:, 0].rearrange("e (q r) n -> r q e n", r=4)
-        for r in range(4):
-            nc.sync.dma_start(w_planes[r:P:32, :, :].bitcast(I32), scale_rows[r].bitcast(I32))
+
+        def load_scales(e0, e1):
+            for r in range(4):
+                nc.sync.dma_start(w_planes[r:P:32, e0:e1, :].bitcast(I32), scale_rows[r][:, e0:e1, :].bitcast(I32))
 
         w_codes = [keep.tile([P, EXPERTS_PER_CHUNK, N], U32, name="w_codes%d" % c, align_bytes=64) for c in range(CHUNKS)]
 
@@ -68,9 +70,12 @@ def tile_routed_moe_kernel(tc, xT, w_words, w_scales, b, gate, offs, out):
             nc.sync.dma_start(gates[k][:], gate_rows[:, :, j0 : j0 + n])
 
         bias = keep.tile([P, BLOCKS, E], F32, name="bias")
+        load_scales(0, EXPERTS_PER_CHUNK)
         load_codes(0)
         nc.sync.dma_start(bias[:], b.rearrange("(m p) e -> p m e", p=P))
-        load_gate(0)
+        for m in range(BLOCKS):
+            nc.sync.dma_start(gates[0][:, m, :], gate_rows[:, m, 0:CHUNK])
+        load_scales(EXPERTS_PER_CHUNK, E)
         load_codes(1)
         load_gate(1)
         load_codes(2)

@@ -69,17 +69,28 @@ def tile_routed_moe_kernel(tc, xT, w_words, w_scales, b, gate, offs, out):
             j0, n = groups[k]
             nc.sync.dma_start(gates[k][:], gate_rows[:, :, j0 : j0 + n])
 
-        bias = keep.tile([P, BLOCKS, E], F32, name="bias")
+        bias_rows = b.rearrange("(m p) e -> p m e", p=P)
+        bias = [
+            keep.tile([P, BLOCKS, EXPERTS_PER_CHUNK], F32, name="bias%d" % c, tag=("turn%d" % c if c < 2 else "bias%d" % c), align_bytes=64)
+            for c in range(CHUNKS)
+        ]
+
+        def load_bias(c):
+            nc.sync.dma_start(bias[c][:], bias_rows[:, :, c * EXPERTS_PER_CHUNK : (c + 1) * EXPERTS_PER_CHUNK])
+
         load_scales(0, EXPERTS_PER_CHUNK)
         load_codes(0)
-        nc.sync.dma_start(bias[:], b.rearrange("(m p) e -> p m e", p=P))
+        load_bias(0)
         for m in range(BLOCKS):
             nc.sync.dma_start(gates[0][:, m, :], gate_rows[:, m, 0:CHUNK])
         load_scales(EXPERTS_PER_CHUNK, E)
         load_codes(1)
+        load_bias(1)
         load_gate(1)
         load_codes(2)
+        load_bias(2)
         load_codes(3)
+        load_bias(3)
         load_gate(2)
 
         zero = keep.tile([P, 1], F32, name="zero")
@@ -91,7 +102,7 @@ def tile_routed_moe_kernel(tc, xT, w_words, w_scales, b, gate, offs, out):
 
         grouped01 = keep.tile([P, HALF, PACK], BF16, name="grouped01", align_bytes=64)
         x_codes = [
-            keep.tile([P, CHUNK], U32, name="x_codes%d" % c, tag=("turn%d" % c if c < 2 else "x_codes%d" % c), align_bytes=64)
+            keep.tile([P, CHUNK], U32, name="x_codes%d" % c, align_bytes=64)
             for c in range(CHUNKS)
         ]
         late = {}
@@ -148,12 +159,11 @@ def tile_routed_moe_kernel(tc, xT, w_words, w_scales, b, gate, offs, out):
             for m in range(BLOCKS):
                 acc = sums[(c, m)]
                 for i in range(EXPERTS_PER_CHUNK):
-                    e = c * EXPERTS_PER_CHUNK + i
                     nc.scalar.activation(
                         out=y[k][:, m, col0 + i * C : col0 + (i + 1) * C],
                         in_=acc[:, i, :],
                         func=RELU,
-                        bias=bias[:, m, e : e + 1],
+                        bias=bias[c][:, m, i : i + 1],
                         scale=1.0,
                     )
 

@@ -13,6 +13,8 @@ U16 = mybir.dt.uint16
 U8 = mybir.dt.uint8
 FP8X4 = mybir.dt.float8_e4m3fn_x4
 MULT = mybir.AluOpType.mult
+ADD = mybir.AluOpType.add
+MAX = mybir.AluOpType.max
 RELU = mybir.ActivationFunctionType.Relu
 COPY = mybir.ActivationFunctionType.Copy
 
@@ -159,13 +161,23 @@ def tile_routed_moe_kernel(tc, xT, w_words, w_scales, b, gate, offs, out):
             for m in range(BLOCKS):
                 acc = sums[(c, m)]
                 for i in range(EXPERTS_PER_CHUNK):
-                    nc.scalar.activation(
-                        out=y[k][:, m, col0 + i * C : col0 + (i + 1) * C],
-                        in_=acc[:, i, :],
-                        func=RELU,
-                        bias=bias[c][:, m, i : i + 1],
-                        scale=1.0,
-                    )
+                    if c == 0 and m == 0:
+                        nc.vector.tensor_scalar(
+                            out=y[k][:, m, col0 + i * C : col0 + (i + 1) * C],
+                            in0=acc[:, i, :],
+                            scalar1=bias[c][:, m, i : i + 1],
+                            scalar2=0.0,
+                            op0=ADD,
+                            op1=MAX,
+                        )
+                    else:
+                        nc.scalar.activation(
+                            out=y[k][:, m, col0 + i * C : col0 + (i + 1) * C],
+                            in_=acc[:, i, :],
+                            func=RELU,
+                            bias=bias[c][:, m, i : i + 1],
+                            scale=1.0,
+                        )
 
         def put_back(k, m, first=0, n=None):
             n = groups[k][1] if n is None else n

@@ -102,23 +102,25 @@ def tile_routed_moe_kernel(tc, xT, w_words, w_scales, b, gate, offs, out):
             nc.gpsimd.memset(windows[m][:], 0.0)
         nc.scalar.copy(out=windows[3][:], in_=zero[:, 0:1].to_broadcast([P, T]))
 
-        grouped01 = keep.tile([P, HALF, PACK], BF16, name="grouped01", align_bytes=64)
+        picked = keep.tile([P, PACK, HALF], F32, name="picked", tag="stage")
+        grouped = [keep.tile([P, CHUNK, PACK], BF16, name="grouped%d" % c, align_bytes=64) for c in range(2)]
         x_codes = [
             keep.tile([P, CHUNK], U32, name="x_codes%d" % c, align_bytes=64)
             for c in range(CHUNKS)
         ]
         late = {}
         x_planes = [keep.tile([P, CHUNK], U8, name="x_planes%d" % c, align_bytes=64) for c in range(CHUNKS)]
-        rounded = [keep.tile([P, T], BF16, name="rounded%d" % t) for t in range(PACK)]
+        rounded = {}
 
-        def vector_gather(t, j0, n):
-            nc.vector.tensor_copy(
-                out=grouped01[:, j0 : j0 + n, t],
-                in_=planes[t][:].indirect(offsets[:, j0 // 16 : (j0 + n) // 16]),
-            )
+        def vector_gather(t):
+            nc.vector.tensor_copy(out=picked[:, t, :], in_=planes[t][:].indirect(offsets[:, 0 : HALF // 16]))
 
         def cast(t):
+            rounded[t] = keep.tile([P, T], BF16, name="rounded%d" % t, tag=("stage" if t == 3 else "rounded%d" % t))
             nc.scalar.copy(out=rounded[t][:], in_=planes[t][:])
+
+        def interleave(c, engine):
+            engine(out=grouped[c][:], in_=picked[:, :, c * CHUNK : (c + 1) * CHUNK].rearrange("p t n -> p n t"))
 
         def scalar_gathers(c):
             late[c] = keep.tile([P, CHUNK, PACK], BF16, name="late%d" % c, tag="turn%d" % (c - 2), align_bytes=64)
@@ -130,7 +132,7 @@ def tile_routed_moe_kernel(tc, xT, w_words, w_scales, b, gate, offs, out):
                 )
 
         def quantise(c):
-            values = grouped01[:, c * CHUNK : (c + 1) * CHUNK, :] if c < 2 else late[c][:]
+            values = grouped[c][:] if c < 2 else late[c][:]
             nc.vector.quantize_mx(
                 out=x_codes[c][:].bitcast(FP8X4),
                 scales=x_planes[c][:],
@@ -192,10 +194,12 @@ def tile_routed_moe_kernel(tc, xT, w_words, w_scales, b, gate, offs, out):
         out_blocks = out.rearrange("(m p) t -> m p t", p=P)
 
         for t in (0, 1, 2):
-            vector_gather(t, 0, HALF)
+            vector_gather(t)
             cast(t)
+        vector_gather(3)
+        interleave(0, nc.vector.tensor_copy)
+        interleave(1, nc.scalar.copy)
         cast(3)
-        vector_gather(3, 0, HALF)
         for c in (0, 1):
             quantise(c)
             multiply(c)

@@ -120,7 +120,10 @@ def tile_routed_moe_kernel(tc, xT, w_words, w_scales, b, gate, offs, out):
             nc.scalar.copy(out=rounded[t][:], in_=planes[t][:])
 
         def interleave(c, engine):
-            engine(out=grouped[c][:], in_=picked[:, :, c * CHUNK : (c + 1) * CHUNK].rearrange("p t n -> p n t"))
+            engine(
+                out=grouped[c][:].rearrange("p (g i) t -> p g t i", i=4),
+                in_=picked[:, :, c * CHUNK : (c + 1) * CHUNK].rearrange("p t (g i) -> p g t i", i=4),
+            )
 
         def scalar_gathers(c):
             late[c] = keep.tile([P, CHUNK, PACK], BF16, name="late%d" % c, tag="turn%d" % (c - 2), align_bytes=64)

@@ -36,14 +36,14 @@ def tile_routed_moe_kernel(tc, xT, w_words, w_scales, b, gate, offs, out):
         psum = ctx.enter_context(tc.psum_pool(name="psum", bufs=1))
 
         offsets = lists.tile([P, SLOTS // 16], U16, name="offsets")
-        nc.sync.dma_start(offsets[:], offs)
-
         x_rows = xT.rearrange("(p t) n -> p t n", t=PACK)
         planes = []
         for t in range(PACK):
             plane = keep.tile([P, T], F32, name="plane%d" % t)
             nc.sync.dma_start(plane[:], x_rows[:, t, :])
             planes.append(plane)
+            if t == 0:
+                nc.sync.dma_start(offsets[:], offs)
 
         w_planes = keep.tile([P, E, N], U8, name="w_planes", align_bytes=64)
         nc.vector.memset(w_planes[:].rearrange("p e n -> p (e n)").bitcast(I32), 0)

@@ -76,14 +76,22 @@ def tile_routed_moe_kernel(tc, xT, w_words, w_scales, b, gate, offs, out):
             keep.tile([P, BLOCKS, EXPERTS_PER_CHUNK], F32, name="bias%d" % c, tag=("turn%d" % c if c < 2 else "bias%d" % c), align_bytes=64)
             for c in range(CHUNKS)
         ]
+        bias_first = keep.tile([P, BLOCKS - 1, EXPERTS_PER_CHUNK], F32, name="bias_first", tag="hold", align_bytes=64)
 
         def load_bias(c):
             nc.sync.dma_start(bias[c][:], bias_rows[:, :, c * EXPERTS_PER_CHUNK : (c + 1) * EXPERTS_PER_CHUNK])
 
+        def bias_of(c, m, i):
+            if c == 0 and m < BLOCKS - 1:
+                return bias_first[:, m, i : i + 1]
+            return bias[c][:, m, i : i + 1]
+
         load_scales(0, EXPERTS_PER_CHUNK)
         load_codes(0)
+        nc.sync.dma_start(bias_first[:], bias_rows[:, 0 : BLOCKS - 1, 0:EXPERTS_PER_CHUNK])
+        nc.sync.dma_start(gates[0][:, 0, :], gate_rows[:, 0, 0:CHUNK])
         load_bias(0)
-        for m in range(BLOCKS):
+        for m in range(1, BLOCKS):
             nc.sync.dma_start(gates[0][:, m, :], gate_rows[:, m, 0:CHUNK])
         load_scales(EXPERTS_PER_CHUNK, E)
         load_codes(1)
@@ -102,7 +110,8 @@ def tile_routed_moe_kernel(tc, xT, w_words, w_scales, b, gate, offs, out):
             nc.gpsimd.memset(windows[m][:], 0.0)
         nc.scalar.copy(out=windows[3][:], in_=zero[:, 0:1].to_broadcast([P, T]))
 
-        picked = keep.tile([P, PACK, HALF], F32, name="picked", tag="stage")
+        low = keep.tile([P, 2, SLOTS], F32, name="low")
+        high = keep.tile([P, 2, CHUNK], F32, name="high")
         grouped = [keep.tile([P, CHUNK, PACK], BF16, name="grouped%d" % c, align_bytes=64) for c in range(2)]
         x_codes = [
             keep.tile([P, CHUNK], U32, name="x_codes%d" % c, align_bytes=64)
@@ -113,21 +122,30 @@ def tile_routed_moe_kernel(tc, xT, w_words, w_scales, b, gate, offs, out):
         rounded = {}
 
         def vector_gather(t):
-            nc.vector.tensor_copy(out=picked[:, t, :], in_=planes[t][:].indirect(offsets[:, 0 : HALF // 16]))
+            if t < 2:
+                for h in range(2):
+                    nc.vector.tensor_copy(
+                        out=low[:, t, h * HALF : (h + 1) * HALF],
+                        in_=planes[t][:].indirect(offsets[:, h * HALF // 16 : (h + 1) * HALF // 16]),
+                    )
+            else:
+                nc.vector.tensor_copy(out=grouped[0][:, :, t], in_=planes[t][:].indirect(offsets[:, 0 : CHUNK // 16]))
+                nc.vector.tensor_copy(out=high[:, t - 2, :], in_=planes[t][:].indirect(offsets[:, CHUNK // 16 : HALF // 16]))
+
+        def lay_low(values, c):
+            nc.scalar.copy(out=values[:, :, 0:2], in_=low[:, :, c * CHUNK : (c + 1) * CHUNK].rearrange("p t n -> p n t"))
 
         def cast(t):
-            rounded[t] = keep.tile([P, T], BF16, name="rounded%d" % t, tag=("stage" if t == 3 else "rounded%d" % t))
+            rounded[t] = keep.tile([P, T], BF16, name="rounded%d" % t, tag=("hold" if t == 3 else "rounded%d" % t), align_bytes=64)
             nc.scalar.copy(out=rounded[t][:], in_=planes[t][:])
 
-        def interleave(c, engine):
-            engine(
-                out=grouped[c][:].rearrange("p (g i) t -> p g t i", i=4),
-                in_=picked[:, :, c * CHUNK : (c + 1) * CHUNK].rearrange("p t (g i) -> p g t i", i=4),
-            )
+        def lay_high():
+            nc.scalar.copy(out=grouped[1][:, :, 2:4], in_=high[:].rearrange("p t n -> p n t"))
 
         def scalar_gathers(c):
             late[c] = keep.tile([P, CHUNK, PACK], BF16, name="late%d" % c, tag="turn%d" % (c - 2), align_bytes=64)
-            for t in range(PACK):
+            lay_low(late[c], c)
+            for t in (2, 3):
                 nc.scalar.activation(
                     out=late[c][:, :, t],
                     in_=rounded[t][:].indirect(offsets[:, c * CHUNK // 16 : (c + 1) * CHUNK // 16]),
@@ -170,7 +188,7 @@ def tile_routed_moe_kernel(tc, xT, w_words, w_scales, b, gate, offs, out):
                         nc.vector.tensor_scalar(
                             out=y[k][:, m, col0 + i * C : col0 + (i + 1) * C],
                             in0=acc[:, i, :],
-                            scalar1=bias[c][:, m, i : i + 1],
+                            scalar1=bias_of(c, m, i),
                             scalar2=0.0,
                             op0=ADD,
                             op1=MAX,
@@ -180,7 +198,7 @@ def tile_routed_moe_kernel(tc, xT, w_words, w_scales, b, gate, offs, out):
                             out=y[k][:, m, col0 + i * C : col0 + (i + 1) * C],
                             in_=acc[:, i, :],
                             func=RELU,
-                            bias=bias[c][:, m, i : i + 1],
+                            bias=bias_of(c, m, i),
                             scale=1.0,
                         )
 
@@ -196,17 +214,20 @@ def tile_routed_moe_kernel(tc, xT, w_words, w_scales, b, gate, offs, out):
 
         out_blocks = out.rearrange("(m p) t -> m p t", p=P)
 
-        for t in (0, 1, 2):
-            vector_gather(t)
-            cast(t)
+        vector_gather(0)
+        vector_gather(1)
+        lay_low(grouped[0], 0)
+        lay_low(grouped[1], 1)
+        vector_gather(2)
+        cast(2)
         vector_gather(3)
-        interleave(0, nc.vector.tensor_copy)
-        interleave(1, nc.scalar.copy)
-        cast(3)
+        lay_high()
         for c in (0, 1):
             quantise(c)
             multiply(c)
             bias_relu(c)
+            if c == 0:
+                cast(3)
         for c in (2, 3):
             scalar_gathers(c)
             quantise(c)

@@ -106,9 +106,10 @@ def tile_routed_moe_kernel(tc, xT, w_words, w_scales, b, gate, offs, out):
         zero = keep.tile([P, 1], F32, name="zero")
         nc.gpsimd.memset(zero[:], 0.0)
         windows = [keep.tile([P, T], F32, name="window%d" % m) for m in range(BLOCKS)]
-        for m in (0, 1, 2):
+        for m in (0, 1):
             nc.gpsimd.memset(windows[m][:], 0.0)
-        nc.scalar.copy(out=windows[3][:], in_=zero[:, 0:1].to_broadcast([P, T]))
+        for m in (2, 3):
+            nc.scalar.copy(out=windows[m][:], in_=zero[:, 0:1].to_broadcast([P, T]))
 
         low = keep.tile([P, 2, SLOTS], F32, name="low")
         high = keep.tile([P, 2, CHUNK], F32, name="high")

@@ -72,35 +72,44 @@ def tile_routed_moe_kernel(tc, xT, w_words, w_scales, b, gate, offs, out):
             nc.sync.dma_start(gates[k][:], gate_rows[:, :, j0 : j0 + n])
 
         bias_rows = b.rearrange("(m p) e -> p m e", p=P)
-        bias = [
-            keep.tile([P, BLOCKS, EXPERTS_PER_CHUNK], F32, name="bias%d" % c, tag=("turn%d" % c if c < 2 else "bias%d" % c), align_bytes=64)
+        head_tags = {0: "turn1", 1: "turn2"}
+        tail_tags = {1: "turn3"}
+        bias_head = [
+            keep.tile([P, BLOCKS - 1, EXPERTS_PER_CHUNK], F32, name="bias_head%d" % c, tag=head_tags.get(c, "bias_head%d" % c), align_bytes=64)
             for c in range(CHUNKS)
         ]
-        bias_first = keep.tile([P, BLOCKS - 1, EXPERTS_PER_CHUNK], F32, name="bias_first", tag="hold", align_bytes=64)
+        bias_tail = [
+            keep.tile([P, 1, EXPERTS_PER_CHUNK], F32, name="bias_tail%d" % c, tag=tail_tags.get(c, "bias_tail%d" % c), align_bytes=64)
+            for c in range(CHUNKS)
+        ]
 
-        def load_bias(c):
-            nc.sync.dma_start(bias[c][:], bias_rows[:, :, c * EXPERTS_PER_CHUNK : (c + 1) * EXPERTS_PER_CHUNK])
+        def load_bias_head(c):
+            nc.sync.dma_start(bias_head[c][:], bias_rows[:, 0 : BLOCKS - 1, c * EXPERTS_PER_CHUNK : (c + 1) * EXPERTS_PER_CHUNK])
+
+        def load_bias_tail(c):
+            nc.sync.dma_start(bias_tail[c][:], bias_rows[:, BLOCKS - 1 : BLOCKS, c * EXPERTS_PER_CHUNK : (c + 1) * EXPERTS_PER_CHUNK])
 
         def bias_of(c, m, i):
-            if c == 0 and m < BLOCKS - 1:
-                return bias_first[:, m, i : i + 1]
-            return bias[c][:, m, i : i + 1]
+            if m < BLOCKS - 1:
+                return bias_head[c][:, m, i : i + 1]
+            return bias_tail[c][:, 0, i : i + 1]
 
         load_scales(0, EXPERTS_PER_CHUNK)
         load_codes(0)
-        nc.sync.dma_start(bias_first[:], bias_rows[:, 0 : BLOCKS - 1, 0:EXPERTS_PER_CHUNK])
+        load_bias_head(0)
         nc.sync.dma_start(gates[0][:, 0, :], gate_rows[:, 0, 0:CHUNK])
-        load_bias(0)
+        load_bias_tail(0)
         for m in range(1, BLOCKS):
             nc.sync.dma_start(gates[0][:, m, :], gate_rows[:, m, 0:CHUNK])
         load_scales(EXPERTS_PER_CHUNK, E)
         load_codes(1)
-        load_bias(1)
+        load_bias_head(1)
+        load_bias_tail(1)
         load_gate(1)
-        load_codes(2)
-        load_bias(2)
-        load_codes(3)
-        load_bias(3)
+        for c in (2, 3):
+            load_codes(c)
+            load_bias_head(c)
+            load_bias_tail(c)
         load_gate(2)
 
         zero = keep.tile([P, 1], F32, name="zero")
@@ -112,53 +121,43 @@ def tile_routed_moe_kernel(tc, xT, w_words, w_scales, b, gate, offs, out):
             nc.scalar.copy(out=windows[m][:], in_=zero[:, 0:1].to_broadcast([P, T]))
 
         low = keep.tile([P, 2, SLOTS], F32, name="low")
-        high = keep.tile([P, 2, CHUNK], F32, name="high")
-        grouped = [keep.tile([P, CHUNK, PACK], BF16, name="grouped%d" % c, align_bytes=64) for c in range(2)]
-        x_codes = [
-            keep.tile([P, CHUNK], U32, name="x_codes%d" % c, align_bytes=64)
-            for c in range(CHUNKS)
-        ]
-        late = {}
+        values = {0: keep.tile([P, CHUNK, PACK], BF16, name="values0", align_bytes=64)}
+        x_codes = [keep.tile([P, CHUNK], U32, name="x_codes%d" % c, align_bytes=64) for c in range(CHUNKS)]
         x_planes = [keep.tile([P, CHUNK], U8, name="x_planes%d" % c, align_bytes=64) for c in range(CHUNKS)]
         rounded = {}
 
-        def vector_gather(t):
-            if t < 2:
-                for h in range(2):
-                    nc.vector.tensor_copy(
-                        out=low[:, t, h * HALF : (h + 1) * HALF],
-                        in_=planes[t][:].indirect(offsets[:, h * HALF // 16 : (h + 1) * HALF // 16]),
-                    )
-            else:
-                nc.vector.tensor_copy(out=grouped[0][:, :, t], in_=planes[t][:].indirect(offsets[:, 0 : CHUNK // 16]))
-                nc.vector.tensor_copy(out=high[:, t - 2, :], in_=planes[t][:].indirect(offsets[:, CHUNK // 16 : HALF // 16]))
+        def gather_low(t):
+            for h in range(2):
+                nc.vector.tensor_copy(
+                    out=low[:, t, h * HALF : (h + 1) * HALF],
+                    in_=planes[t][:].indirect(offsets[:, h * HALF // 16 : (h + 1) * HALF // 16]),
+                )
 
-        def lay_low(values, c):
-            nc.scalar.copy(out=values[:, :, 0:2], in_=low[:, :, c * CHUNK : (c + 1) * CHUNK].rearrange("p t n -> p n t"))
+        def lay_low(c):
+            nc.scalar.copy(out=values[c][:, :, 0:2], in_=low[:, :, c * CHUNK : (c + 1) * CHUNK].rearrange("p t n -> p n t"))
+
+        def gather_first(t):
+            nc.vector.tensor_copy(out=values[0][:, :, t], in_=planes[t][:].indirect(offsets[:, 0 : CHUNK // 16]))
 
         def cast(t):
-            rounded[t] = keep.tile([P, T], BF16, name="rounded%d" % t, tag=("hold" if t == 3 else "rounded%d" % t), align_bytes=64)
+            rounded[t] = keep.tile([P, T], BF16, name="rounded%d" % t)
             nc.scalar.copy(out=rounded[t][:], in_=planes[t][:])
 
-        def lay_high():
-            nc.scalar.copy(out=grouped[1][:, :, 2:4], in_=high[:].rearrange("p t n -> p n t"))
-
-        def scalar_gathers(c):
-            late[c] = keep.tile([P, CHUNK, PACK], BF16, name="late%d" % c, tag="turn%d" % (c - 2), align_bytes=64)
-            lay_low(late[c], c)
+        def scalar_chunk(c):
+            values[c] = keep.tile([P, CHUNK, PACK], BF16, name="values%d" % c, tag="turn%d" % c, align_bytes=64)
+            lay_low(c)
             for t in (2, 3):
                 nc.scalar.activation(
-                    out=late[c][:, :, t],
+                    out=values[c][:, :, t],
                     in_=rounded[t][:].indirect(offsets[:, c * CHUNK // 16 : (c + 1) * CHUNK // 16]),
                     func=COPY,
                 )
 
         def quantise(c):
-            values = grouped[c][:] if c < 2 else late[c][:]
             nc.vector.quantize_mx(
                 out=x_codes[c][:].bitcast(FP8X4),
                 scales=x_planes[c][:],
-                in_=values.rearrange("p n t -> p (n t)"),
+                in_=values[c][:].rearrange("p n t -> p (n t)"),
             )
 
         sums = {}
@@ -215,22 +214,17 @@ def tile_routed_moe_kernel(tc, xT, w_words, w_scales, b, gate, offs, out):
 
         out_blocks = out.rearrange("(m p) t -> m p t", p=P)
 
-        vector_gather(0)
-        vector_gather(1)
-        lay_low(grouped[0], 0)
-        lay_low(grouped[1], 1)
-        vector_gather(2)
-        cast(2)
-        vector_gather(3)
-        lay_high()
-        for c in (0, 1):
-            quantise(c)
-            multiply(c)
-            bias_relu(c)
-            if c == 0:
-                cast(3)
-        for c in (2, 3):
-            scalar_gathers(c)
+        gather_low(0)
+        gather_low(1)
+        lay_low(0)
+        for t in (2, 3):
+            gather_first(t)
+            cast(t)
+        quantise(0)
+        multiply(0)
+        bias_relu(0)
+        for c in (1, 2, 3):
+            scalar_chunk(c)
             quantise(c)
             multiply(c)
             bias_relu(c)

@@ -55,11 +55,11 @@ def tile_routed_moe_kernel(tc, xT, w_words, w_scales, b, gate, offs, out):
 
         w_codes = [keep.tile([P, EXPERTS_PER_CHUNK, N], U32, name="w_codes%d" % c, align_bytes=64) for c in range(CHUNKS)]
 
-        def load_codes(c):
+        def load_codes(c, n0=0, n1=N):
             e0 = c * EXPERTS_PER_CHUNK
             nc.sync.dma_start(
-                w_codes[c][:].bitcast(I32),
-                w_words[e0 : e0 + EXPERTS_PER_CHUNK, 0].rearrange("e p n r -> p e (n r)").bitcast(I32),
+                w_codes[c][:, :, n0:n1].bitcast(I32),
+                w_words[e0 : e0 + EXPERTS_PER_CHUNK, 0, :, n0:n1, :].rearrange("e p n r -> p e (n r)").bitcast(I32),
             )
 
         groups = [(0, CHUNK), (CHUNK, CHUNK), (2 * CHUNK, 2 * CHUNK)]
@@ -95,9 +95,10 @@ def tile_routed_moe_kernel(tc, xT, w_words, w_scales, b, gate, offs, out):
             return bias_tail[c][:, 0, i : i + 1]
 
         load_scales(0, EXPERTS_PER_CHUNK)
-        load_codes(0)
+        load_codes(0, 0, N // 2)
         load_bias_head(0)
         nc.sync.dma_start(gates[0][:, 0, :], gate_rows[:, 0, 0:CHUNK])
+        load_codes(0, N // 2, N)
         load_bias_tail(0)
         for m in range(1, BLOCKS):
             nc.sync.dma_start(gates[0][:, m, :], gate_rows[:, m, 0:CHUNK])

@@ -154,11 +154,11 @@ def tile_routed_moe_kernel(tc, xT, w_words, w_scales, b, gate, offs, out):
                     func=COPY,
                 )
 
-        def quantise(c):
+        def quantise(c, first=0, n=CHUNK):
             nc.vector.quantize_mx(
-                out=x_codes[c][:].bitcast(FP8X4),
-                scales=x_planes[c][:],
-                in_=values[c][:].rearrange("p n t -> p (n t)"),
+                out=x_codes[c][:, first : first + n].bitcast(FP8X4),
+                scales=x_planes[c][:, first : first + n],
+                in_=values[c][:, first : first + n, :].rearrange("p n t -> p (n t)"),
             )
 
         sums = {}
@@ -221,7 +221,8 @@ def tile_routed_moe_kernel(tc, xT, w_words, w_scales, b, gate, offs, out):
         for t in (2, 3):
             gather_first(t)
             cast(t)
-        quantise(0)
+        quantise(0, 0, C)
+        quantise(0, C, C)
         multiply(0)
         bias_relu(0)
         for c in (1, 2, 3):

@@ -116,8 +116,8 @@ def tile_routed_moe_kernel(tc, xT, w_words, w_scales, b, gate, offs, out):
         zero = keep.tile([P, 1], F32, name="zero")
         nc.gpsimd.memset(zero[:], 0.0)
         windows = [keep.tile([P, T], F32, name="window%d" % m) for m in range(BLOCKS)]
-        for m in (0, 1):
-            nc.gpsimd.memset(windows[m][:], 0.0)
+        nc.gpsimd.memset(windows[0][:], 0.0)
+        nc.vector.memset(windows[1][:], 0.0)
         for m in (2, 3):
             nc.scalar.copy(out=windows[m][:], in_=zero[:, 0:1].to_broadcast([P, T]))
 

from contextlib import ExitStack

import concourse.mybir as mybir

K, T, E, C, N = 512, 2048, 8, 128, 512
FLOPS = 2 * K * N * E * C

F32 = mybir.dt.float32
BF16 = mybir.dt.bfloat16
I32 = mybir.dt.int32
U32 = mybir.dt.uint32
U16 = mybir.dt.uint16
U8 = mybir.dt.uint8
FP8X4 = mybir.dt.float8_e4m3fn_x4
MULT = mybir.AluOpType.mult
ADD = mybir.AluOpType.add
MAX = mybir.AluOpType.max
RELU = mybir.ActivationFunctionType.Relu
COPY = mybir.ActivationFunctionType.Copy

P = 128
PACK = 4
SLOTS = E * C
CHUNK = 256
CHUNKS = SLOTS // CHUNK
EXPERTS_PER_CHUNK = CHUNK // C
HALF = 512
BLOCKS = N // P


def tile_routed_moe_kernel(tc, xT, w_words, w_scales, b, gate, offs, out):
    nc = tc.nc
    with ExitStack() as ctx:
        lists = ctx.enter_context(tc.tile_pool(name="lists", bufs=1))
        keep = ctx.enter_context(tc.tile_pool(name="keep", bufs=1))
        psum = ctx.enter_context(tc.psum_pool(name="psum", bufs=1))

        offsets = lists.tile([P, SLOTS // 16], U16, name="offsets")
        x_rows = xT.rearrange("(p t) n -> p t n", t=PACK)
        planes = []
        for t in range(PACK):
            plane = keep.tile([P, T], F32, name="plane%d" % t)
            nc.sync.dma_start(plane[:], x_rows[:, t, :])
            planes.append(plane)
            if t == 0:
                nc.sync.dma_start(offsets[:], offs)

        w_planes = keep.tile([P, E, N], U8, name="w_planes", align_bytes=64)
        nc.vector.memset(w_planes[:].rearrange("p e n -> p (e n)").bitcast(I32), 0)
        scale_rows = w_scales[:, 0].rearrange("e (q r) n -> r q e n", r=4)

        def load_scales(e0, e1):
            for r in range(4):
                nc.sync.dma_start(w_planes[r:P:32, e0:e1, :].bitcast(I32), scale_rows[r][:, e0:e1, :].bitcast(I32))

        w_codes = [keep.tile([P, EXPERTS_PER_CHUNK, N], U32, name="w_codes%d" % c, align_bytes=64) for c in range(CHUNKS)]

        def load_codes(c, n0=0, n1=N):
            e0 = c * EXPERTS_PER_CHUNK
            nc.sync.dma_start(
                w_codes[c][:, :, n0:n1].bitcast(I32),
                w_words[e0 : e0 + EXPERTS_PER_CHUNK, 0, :, n0:n1, :].rearrange("e p n r -> p e (n r)").bitcast(I32),
            )

        groups = [(0, CHUNK), (CHUNK, CHUNK), (2 * CHUNK, 2 * CHUNK)]
        gate_rows = gate.rearrange("(m p) j -> p m j", p=P)
        gates = [keep.tile([P, BLOCKS, n], F32, name="gate%d" % k) for k, (j0, n) in enumerate(groups)]
        y = [keep.tile([P, BLOCKS, n], F32, name="y%d" % k) for k, (j0, n) in enumerate(groups)]

        def load_gate(k):
            j0, n = groups[k]
            nc.sync.dma_start(gates[k][:], gate_rows[:, :, j0 : j0 + n])

        bias_rows = b.rearrange("(m p) e -> p m e", p=P)
        head_tags = {0: "turn1", 1: "turn2"}
        tail_tags = {1: "turn3"}
        bias_head = [
            keep.tile([P, BLOCKS - 1, EXPERTS_PER_CHUNK], F32, name="bias_head%d" % c, tag=head_tags.get(c, "bias_head%d" % c), align_bytes=64)
            for c in range(CHUNKS)
        ]
        bias_tail = [
            keep.tile([P, 1, EXPERTS_PER_CHUNK], F32, name="bias_tail%d" % c, tag=tail_tags.get(c, "bias_tail%d" % c), align_bytes=64)
            for c in range(CHUNKS)
        ]

        def load_bias_head(c):
            nc.sync.dma_start(bias_head[c][:], bias_rows[:, 0 : BLOCKS - 1, c * EXPERTS_PER_CHUNK : (c + 1) * EXPERTS_PER_CHUNK])

        def load_bias_tail(c):
            nc.sync.dma_start(bias_tail[c][:], bias_rows[:, BLOCKS - 1 : BLOCKS, c * EXPERTS_PER_CHUNK : (c + 1) * EXPERTS_PER_CHUNK])

        def bias_of(c, m, i):
            if m < BLOCKS - 1:
                return bias_head[c][:, m, i : i + 1]
            return bias_tail[c][:, 0, i : i + 1]

        load_scales(0, EXPERTS_PER_CHUNK)
        load_codes(0, 0, N // 2)
        load_bias_head(0)
        nc.sync.dma_start(gates[0][:, 0, :], gate_rows[:, 0, 0:CHUNK])
        load_codes(0, N // 2, N)
        load_bias_tail(0)
        for m in range(1, BLOCKS):
            nc.sync.dma_start(gates[0][:, m, :], gate_rows[:, m, 0:CHUNK])
        load_scales(EXPERTS_PER_CHUNK, E)
        load_codes(1)
        load_bias_head(1)
        load_bias_tail(1)
        load_gate(1)
        for c in (2, 3):
            load_codes(c)
            load_bias_head(c)
            load_bias_tail(c)
        load_gate(2)

        zero = keep.tile([P, 1], F32, name="zero")
        nc.gpsimd.memset(zero[:], 0.0)
        windows = [keep.tile([P, T], F32, name="window%d" % m) for m in range(BLOCKS)]
        nc.gpsimd.memset(windows[0][:], 0.0)
        nc.vector.memset(windows[1][:], 0.0)
        for m in (2, 3):
            nc.scalar.copy(out=windows[m][:], in_=zero[:, 0:1].to_broadcast([P, T]))

        low = keep.tile([P, 2, SLOTS], F32, name="low")
        values = {0: keep.tile([P, CHUNK, PACK], BF16, name="values0", align_bytes=64)}
        x_codes = [keep.tile([P, CHUNK], U32, name="x_codes%d" % c, align_bytes=64) for c in range(CHUNKS)]
        x_planes = [keep.tile([P, CHUNK], U8, name="x_planes%d" % c, align_bytes=64) for c in range(CHUNKS)]
        rounded = {}

        def gather_low(t):
            for h in range(2):
                nc.vector.tensor_copy(
                    out=low[:, t, h * HALF : (h + 1) * HALF],
                    in_=planes[t][:].indirect(offsets[:, h * HALF // 16 : (h + 1) * HALF // 16]),
                )

        def lay_low(c):
            nc.scalar.copy(out=values[c][:, :, 0:2], in_=low[:, :, c * CHUNK : (c + 1) * CHUNK].rearrange("p t n -> p n t"))

        def gather_first(t):
            nc.vector.tensor_copy(out=values[0][:, :, t], in_=planes[t][:].indirect(offsets[:, 0 : CHUNK // 16]))

        def cast(t):
            rounded[t] = keep.tile([P, T], BF16, name="rounded%d" % t)
            nc.scalar.copy(out=rounded[t][:], in_=planes[t][:])

        def scalar_chunk(c):
            values[c] = keep.tile([P, CHUNK, PACK], BF16, name="values%d" % c, tag="turn%d" % c, align_bytes=64)
            lay_low(c)
            for t in (2, 3):
                nc.scalar.activation(
                    out=values[c][:, :, t],
                    in_=rounded[t][:].indirect(offsets[:, c * CHUNK // 16 : (c + 1) * CHUNK // 16]),
                    func=COPY,
                )

        def quantise(c, first=0, n=CHUNK):
            nc.vector.quantize_mx(
                out=x_codes[c][:, first : first + n].bitcast(FP8X4),
                scales=x_planes[c][:, first : first + n],
                in_=values[c][:, first : first + n, :].rearrange("p n t -> p (n t)"),
            )

        sums = {}

        def multiply(c):
            for m in range(BLOCKS):
                acc = psum.tile([P, EXPERTS_PER_CHUNK, C], F32, name="acc%d_%d" % (c % 2, m))
                sums[(c, m)] = acc
                for i in range(EXPERTS_PER_CHUNK):
                    e = c * EXPERTS_PER_CHUNK + i
                    nc.tensor.matmul_mx(
                        out=acc[:, i, :],
                        lhsT=w_codes[c][:, i, m * P : (m + 1) * P].bitcast(FP8X4),
                        lhsT_scale=w_planes[:, e, m * P : (m + 1) * P],
                        rhs=x_codes[c][:, i * C : (i + 1) * C].bitcast(FP8X4),
                        rhs_scale=x_planes[c][:, i * C : (i + 1) * C],
                        start=True,
                        stop=True,
                    )

        def bias_relu(c):
            k = min(c, 2)
            col0 = c * CHUNK - groups[k][0]
            for m in range(BLOCKS):
                acc = sums[(c, m)]
                for i in range(EXPERTS_PER_CHUNK):
                    if c == 0 and m == 0:
                        nc.vector.tensor_scalar(
                            out=y[k][:, m, col0 + i * C : col0 + (i + 1) * C],
                            in0=acc[:, i, :],
                            scalar1=bias_of(c, m, i),
                            scalar2=0.0,
                            op0=ADD,
                            op1=MAX,
                        )
                    else:
                        nc.scalar.activation(
                            out=y[k][:, m, col0 + i * C : col0 + (i + 1) * C],
                            in_=acc[:, i, :],
                            func=RELU,
                            bias=bias_of(c, m, i),
                            scale=1.0,
                        )

        def put_back(k, m, first=0, n=None):
            n = groups[k][1] if n is None else n
            j0 = groups[k][0] + first
            nc.vector.tensor_tensor(
                out=windows[m][:].indirect(offsets[:, j0 // 16 : (j0 + n) // 16]),
                in0=y[k][:, m, first : first + n],
                in1=gates[k][:, m, first : first + n],
                op=MULT,
            )

        out_blocks = out.rearrange("(m p) t -> m p t", p=P)

        gather_low(0)
        gather_low(1)
        lay_low(0)
        for t in (2, 3):
            gather_first(t)
            cast(t)
        quantise(0, 0, C)
        quantise(0, C, C)
        multiply(0)
        bias_relu(0)
        for c in (1, 2, 3):
            scalar_chunk(c)
            quantise(c)
            multiply(c)
            bias_relu(c)
        for k in (0, 1):
            for m in range(BLOCKS):
                put_back(k, m)
        for m in range(BLOCKS):
            if m == 0:
                put_back(2, m, 0, CHUNK)
                put_back(2, m, CHUNK, CHUNK)
            else:
                put_back(2, m)
            nc.sync.dma_start(out_blocks[m], windows[m][:])
